import numpy as np
import ml_dtypes


def mxq(x, axis, fmt="e4m3"):
    dtype, down = {"e4m3": (ml_dtypes.float8_e4m3fn, 7), "e5m2": (ml_dtypes.float8_e5m2, 14)}[fmt]
    v = np.moveaxis(np.asarray(x, np.float32).astype(ml_dtypes.bfloat16).astype(np.float64), axis, -1)
    blocks = v.reshape(v.shape[:-1] + (-1, 32))
    amax = np.abs(blocks).max(-1, keepdims=True)
    byte = np.maximum(np.where(amax > 0, np.frexp(amax)[1] - 1 + 127, 0) - down, 1)
    scale = np.exp2(byte - 127.0)
    codes = (blocks / scale).astype(np.float32).astype(dtype).astype(np.float64)
    return np.moveaxis((codes * scale).reshape(v.shape), -1, axis)


WIDE = False


def mx_kscale(k):
    if not WIDE:
        return np.ones(k)
    levels = np.array([10, -10, 5, -5, 0])
    if k % 512:
        return np.exp2(np.random.permutation(np.resize(levels, k // 32))).repeat(32)
    a = np.empty((k // 512, 16))
    for p in range(k // 512):
        a[p, :8] = np.random.permutation(np.resize(levels, 8))
        for g in range(8):
            far = levels[np.abs(levels - a[p, g]) >= 10]
            a[p, g + 8] = far[np.random.randint(len(far))]
    return np.exp2(a.ravel()).repeat(32)


def f64(x):
    return np.asarray(x).astype(np.float64)


def striped(idx):
    return np.tile(idx.reshape(-1, 16).T, (8, 1)).astype(np.uint16)


def unstriped(offs):
    return offs[:16].T.reshape(-1).astype(np.int64)


def striped8(idx):
    return np.concatenate([x.reshape(-1, 16).T for x in idx]).astype(np.uint16)


def runs(offs, k):
    lists = np.stack([offs[16 * r : 16 * r + 16].T.reshape(-1) for r in range(8)]).astype(np.int64)
    return lists[np.arange(k) % 512 // 64]


def pack_weight(w):
    k, n = w.shape
    w = f64(np.asarray(w, np.float32).astype(ml_dtypes.bfloat16)).reshape(k // 32, 32, n)
    amax = np.abs(w).max(1)
    byte = np.clip(np.where(amax > 0, np.frexp(amax)[1] - 1 + 127 - 7, 1), 1, 254)
    scaled = (w * np.exp2(127.0 - byte)[:, None, :]).reshape(k, n).astype(np.float32)
    words = np.ascontiguousarray(scaled.reshape(k // 512, 128, 4, n).transpose(0, 1, 3, 2)).astype(ml_dtypes.float8_e4m3fn).view(np.uint8)
    return words, np.ascontiguousarray(byte.astype(np.uint8).reshape(k // 512, 16, n))


def unpack_weight(words, scales):
    g, p, n, _ = words.shape
    vals = np.ascontiguousarray(words).view(ml_dtypes.float8_e4m3fn).astype(np.float64) * np.repeat(np.exp2(scales.astype(np.float64) - 127.0), 8, axis=1)[..., None]
    return vals.transpose(0, 1, 3, 2).reshape(g * 512, n)


def sigmoid(v):
    return 1.0 / (1.0 + np.exp(-np.maximum(v, -700.0)))


K, T, S, N, H, W = 512, 2048, 512, 512, 512, 256


def setup_inputs():
    n = np.random.standard_normal
    s = mx_kscale(K)[:, None]
    u = mx_kscale(H)
    packed_xT = pack_weight(n((K, T)) * s)
    perm = np.stack([np.random.permutation(S) for _ in range(8)])
    return {
        "x_words": packed_xT[0],
        "x_scales": packed_xT[1],
        "w1": (n((K, H)) / np.sqrt(K) / s).astype(np.float32),
        "gn": (np.random.uniform(0.5, 1.5, (H, 1)) * u[:, None]).astype(np.float32),
        "gm": (np.random.uniform(0.5, 1.5, (H, 1)) * u[:, None]).astype(np.float32),
        "w2": (n((H, N)) / np.sqrt(2 * H) / u[:, None]).astype(np.float32),
        "w3": (n((H, N)) / np.sqrt(2 * H) / u[:, None]).astype(np.float32),
        "offs": striped(np.random.permutation(T)[:S]),
        "n1": striped8(perm[:, :W]),
        "n2": striped8(perm[:, W:]),
        "n3": striped8(np.stack([np.random.permutation(S) for _ in range(8)])),
        "n4": striped8(np.stack([np.random.permutation(S) for _ in range(8)])),
        "n5": striped8(np.stack([np.random.permutation(S) for _ in range(8)])),
        "n6": striped8(np.stack([np.random.permutation(S) for _ in range(8)])),
        "n7": striped8(np.stack([np.random.permutation(S) for _ in range(8)])),
    }


def reference(x_words, x_scales, w1, gn, gm, w2, w3, offs, n1, n2, n3, n4, n5, n6, n7):
    xq = unpack_weight(x_words, x_scales)[:, unstriped(offs)]
    y = mxq(f64(w1), 0, "e4m3").T @ xq
    pb = y[np.arange(H)[:, None], runs(n2, H)]
    pa = y[np.arange(H)[:, None], runs(n1, H)]
    rb = pb * sigmoid(pb - pa)
    ra = pa * sigmoid(pa - pb)
    ds = np.zeros((H, S))
    ds[np.arange(H)[:, None], runs(n1, H)] = ra
    dt = ds.copy()
    dt[np.arange(H)[:, None], runs(n2, H)] = rb
    z = f64(gn) * dt
    pa2 = y[np.arange(H)[:, None], runs(n3, H)]
    pb2 = y[np.arange(H)[:, None], runs(n4, H)]
    z2 = f64(gm) * (np.maximum(np.maximum(y, pa2), pb2) - (0.5 * (np.minimum(np.minimum(y, pa2), pb2))))
    h = mxq(f64(w2), 0, "e4m3").T @ mxq(z, 0, "e4m3") + mxq(f64(w3), 0, "e4m3").T @ mxq(z2, 0, "e4m3")
    st = h - (h[np.arange(N)[:, None], runs(n5, N)])
    su = np.maximum(st, st[np.arange(N)[:, None], runs(n6, N)])
    return su + 0.5 * (su[np.arange(N)[:, None], runs(n7, N)])

@@ -1,0 +1,185 @@
+from contextlib import ExitStack
+
+import concourse.mybir as mybir
+
+K, T, S, H, N, W = 512, 2048, 512, 512, 512, 256
+FLOPS = 2 * S * (K * H + 2 * H * N)
+
+F32 = mybir.dt.float32
+BF16 = mybir.dt.bfloat16
+I32 = mybir.dt.int32
+U32 = mybir.dt.uint32
+U16 = mybir.dt.uint16
+U8 = mybir.dt.uint8
+FP8X4 = mybir.dt.float8_e4m3fn_x4
+ALU = mybir.AluOpType
+ACT = mybir.ActivationFunctionType
+
+P = 128
+PACK = 4
+WINDOW = 2 * S
+
+
+def tile_picked_joinduelrangethree_none_p_kernel(
+    tc, x_words, x_scales, w1, gn, gm, w2, w3, offs, n1, n2, n3, n4, n5, n6, n7, out
+):
+    nc = tc.nc
+    with ExitStack() as ctx:
+        keep = ctx.enter_context(tc.tile_pool(name="keep", bufs=1))
+        ring = ctx.enter_context(tc.tile_pool(name="ring", bufs=2))
+        psum = ctx.enter_context(tc.psum_pool(name="psum", bufs=1))
+
+        def load_list(name, dram):
+            tile = keep.tile(list(dram.shape), U16, name=name)
+            nc.sync.dma_start(tile[:], dram)
+            return tile
+
+        def load_weight(name, dram, c0, c1):
+            tile = keep.tile([P, PACK, c1 - c0], F32, name=name)
+            nc.sync.dma_start(tile[:], dram.rearrange("(p j) c -> p j c", j=PACK)[:, :, c0:c1])
+            return tile
+
+        def deal(engine_copy, grouped, raw, c0, c1):
+            engine_copy(
+                out=grouped[:].rearrange("p (t m j) -> p m j t", t=PACK, j=PACK)[:, c0 // PACK : c1 // PACK],
+                in_=raw[:].rearrange("p j (m t) -> p m j t", t=PACK),
+            )
+
+        def mx_tiles(name):
+            return (
+                keep.tile([P, S], U32, name=name + "_codes", align_bytes=64),
+                keep.tile([P, S], U8, name=name + "_scales", align_bytes=64),
+            )
+
+        def quantize(mx, grouped, c0, c1):
+            nc.vector.quantize_mx(
+                out=mx[0][:, c0:c1].bitcast(FP8X4),
+                scales=mx[1][:, c0:c1],
+                in_=grouped[:, PACK * c0 : PACK * c1],
+            )
+
+        def product(bank, w_mx, t, x_mx, start, stop):
+            nc.tensor.matmul_mx(
+                out=bank[:],
+                lhsT=w_mx[0][:, t * P : (t + 1) * P].bitcast(FP8X4),
+                lhsT_scale=w_mx[1][:, t * P : (t + 1) * P],
+                rhs=x_mx[0][:].bitcast(FP8X4),
+                rhs_scale=x_mx[1][:],
+                start=start,
+                stop=stop,
+            )
+
+        x_bytes = keep.tile([P, T], U8, name="x_bytes")
+        nc.vector.memset(x_bytes[:].bitcast(I32), 0)
+        offs_t = load_list("offs_t", offs)
+        x_table = keep.tile([P, T], U32, name="x_table")
+        nc.sync.dma_start(x_table[:].bitcast(I32), x_words[0].rearrange("p n t -> p (n t)").bitcast(I32))
+        for q in range(4):
+            nc.scalar.dma_start(
+                x_bytes[32 * q : 32 * q + 4, :].bitcast(I32), x_scales[0][4 * q : 4 * q + 4, :].bitcast(I32)
+            )
+        w1_a = load_weight("w1_a", w1, 0, H // 2)
+        w1_b = load_weight("w1_b", w1, H // 2, H)
+        n1_t = load_list("n1_t", n1)
+        n2_t = load_list("n2_t", n2)
+        n3_t = load_list("n3_t", n3)
+        n4_t = load_list("n4_t", n4)
+        gn_t = keep.tile([P, PACK], F32, name="gn_t")
+        nc.sync.dma_start(gn_t[:], gn.rearrange("(p t) one -> p (t one)", t=PACK))
+        gm_t = keep.tile([P, PACK], F32, name="gm_t")
+        nc.sync.dma_start(gm_t[:], gm.rearrange("(p t) one -> p (t one)", t=PACK))
+        n5_t = load_list("n5_t", n5)
+        n6_t = load_list("n6_t", n6)
+        n7_t = load_list("n7_t", n7)
+        w3_raw = load_weight("w3_raw", w3, 0, N)
+        w2_raw = load_weight("w2_raw", w2, 0, N)
+
+        win_a = [keep.tile([P, WINDOW], F32, name="win_a%d" % t) for t in range(PACK)]
+        win_b = [keep.tile([P, WINDOW], F32, name="win_b%d" % t) for t in range(PACK)]
+        for t in range(PACK):
+            nc.vector.memset(win_a[t][:, S:], 0.0)
+        for t in range(PACK):
+            nc.vector.memset(win_b[t][:, S:], 0.0)
+
+        x_mx = mx_tiles("x")
+        nc.vector.tensor_copy(x_mx[1][:], x_bytes[:].indirect(offs_t[:]))
+        nc.vector.tensor_copy(x_mx[0][:], x_table[:].indirect(offs_t[:]))
+
+        w1_g = keep.tile([P, PACK * H], BF16, name="w1_g", align_bytes=64)
+        deal(nc.scalar.copy, w1_g, w1_a, 0, H // 2)
+        deal(nc.vector.tensor_copy, w1_g, w1_b, H // 2, H)
+        w1_mx = mx_tiles("w1")
+        y_plain = []
+        for t in range(PACK):
+            quantize(w1_mx, w1_g, t * P, (t + 1) * P)
+            bank = psum.tile([P, S], F32, name="y_bank%d" % t)
+            product(bank, w1_mx, t, x_mx, True, True)
+            nc.scalar.copy(out=win_a[t][:, :S], in_=bank[:])
+            plain = keep.tile([P, S], F32, name="y_plain%d" % t)
+            nc.scalar.copy(out=plain[:], in_=bank[:])
+            y_plain.append(plain)
+
+        z_g = keep.tile([P, PACK * S], BF16, name="z_g", align_bytes=64)
+        z2_g = keep.tile([P, PACK * S], BF16, name="z2_g", align_bytes=64)
+        z_view = z_g[:].rearrange("p (j t) -> p j t", t=PACK)
+        z2_view = z2_g[:].rearrange("p (j t) -> p j t", t=PACK)
+        w2_g = keep.tile([P, PACK * N], BF16, name="w2_g", align_bytes=64)
+        w3_g = keep.tile([P, PACK * N], BF16, name="w3_g", align_bytes=64)
+
+        for t in range(PACK):
+            y_win = win_a[t]
+            pair = ring.tile([P, 2, W], F32, name="pair")
+            nc.vector.tensor_copy(pair[:, 0, :], y_win[:].indirect(n1_t[:]))
+            nc.vector.tensor_copy(pair[:, 1, :], y_win[:].indirect(n2_t[:]))
+            diff = ring.tile([P, W], F32, name="diff")
+            nc.vector.tensor_tensor(diff[:], pair[:, 0, :], pair[:, 1, :], ALU.subtract)
+            sig = ring.tile([P, 2, W], F32, name="sig")
+            nc.scalar.activation(sig[:, 0, :], diff[:], ACT.Sigmoid)
+            nc.scalar.activation(sig[:, 1, :], diff[:], ACT.Sigmoid, scale=-1.0)
+
+            d1 = ring.tile([P, S], F32, name="d1")
+            d2 = ring.tile([P, S], F32, name="d2")
+            nc.vector.tensor_tensor(d1[:], y_win[:].indirect(n3_t[:]), y_plain[t][:], ALU.subtract)
+            nc.vector.tensor_tensor(d2[:], y_win[:].indirect(n4_t[:]), y_plain[t][:], ALU.subtract)
+            hi = ring.tile([P, S], F32, name="hi")
+            lo = ring.tile([P, S], F32, name="lo")
+            nc.vector.tensor_tensor(win_b[t][:].indirect(n1_t[:]), pair[:, 0, :], sig[:, 0, :], ALU.mult)
+            nc.vector.scalar_tensor_tensor(hi[:], d1[:], 0.0, d2[:], ALU.max, ALU.max)
+            nc.vector.scalar_tensor_tensor(lo[:], d1[:], 0.0, d2[:], ALU.min, ALU.min)
+            part = ring.tile([P, S], F32, name="part")
+            nc.vector.scalar_tensor_tensor(part[:], y_plain[t][:], 0.5, hi[:], ALU.mult, ALU.add)
+            rng = ring.tile([P, S], F32, name="rng")
+            nc.vector.scalar_tensor_tensor(rng[:], lo[:], -0.5, part[:], ALU.mult, ALU.add)
+            nc.vector.tensor_tensor(win_b[t][:].indirect(n2_t[:]), pair[:, 1, :], sig[:, 1, :], ALU.mult)
+            nc.scalar.activation(z2_view[:, :, t], rng[:], ACT.Copy, scale=gm_t[:, t : t + 1])
+            nc.scalar.activation(z_view[:, :, t], win_b[t][:, :S], ACT.Copy, scale=gn_t[:, t : t + 1])
+            if t == 1:
+                deal(nc.scalar.copy, w3_g, w3_raw, 0, N)
+            if t == 2:
+                deal(nc.scalar.copy, w2_g, w2_raw, 0, N)
+
+        w2_mx, w3_mx, z_mx, z2_mx = mx_tiles("w2"), mx_tiles("w3"), mx_tiles("z"), mx_tiles("z2")
+        quantize(w3_mx, w3_g, 0, N)
+        quantize(w2_mx, w2_g, 0, N)
+        quantize(z2_mx, z2_g, 0, S)
+        quantize(z_mx, z_g, 0, S)
+        banks = [psum.tile([P, S], F32, name="h_bank%d" % t) for t in range(PACK)]
+        for t in range(PACK):
+            product(banks[t], w3_mx, t, z2_mx, True, False)
+        for t in range(PACK):
+            product(banks[t], w2_mx, t, z_mx, False, True)
+
+        for t in range(PACK):
+            nc.scalar.copy(out=win_a[t][:, :S], in_=banks[t][:])
+            nc.scalar.copy(out=y_plain[t][:], in_=banks[t][:])
+            nc.vector.tensor_tensor(win_b[t][:, :S], win_a[t][:].indirect(n5_t[:]), y_plain[t][:], ALU.subtract)
+        for t in range(PACK):
+            far = ring.tile([P, S], F32, name="far")
+            nc.vector.tensor_copy(far[:], win_b[t][:].indirect(n6_t[:]))
+            nc.vector.tensor_tensor(y_plain[t][:], win_b[t][:, :S], far[:], ALU.min)
+            nc.scalar.activation(win_a[t][:, :S], y_plain[t][:], ACT.Copy, scale=-0.5)
+        out_rows = out.rearrange("(p t) n -> p t n", t=PACK)
+        for t in range(PACK):
+            result = keep.tile([P, S], F32, name="result%d" % t)
+            nc.vector.tensor_tensor(result[:], win_a[t][:].indirect(n7_t[:]), y_plain[t][:], ALU.subtract)
+            nc.sync.dma_start(out_rows[:, t, :], result[:])

@@ -1,6 +1,7 @@
 from contextlib import ExitStack
 
 import concourse.mybir as mybir
+from concourse.masks import make_identity
 
 K, T, S, H, N, W = 512, 2048, 512, 512, 512, 256
 FLOPS = 2 * S * (K * H + 2 * H * N)
@@ -18,6 +19,9 @@ ACT = mybir.ActivationFunctionType
 P = 128
 PACK = 4
 WINDOW = 2 * S
+HALF = S // 2
+W1_SPLIT = 256
+W1_VECTOR_END = 416
 
 
 def tile_picked_joinduelrangethree_none_p_kernel(
@@ -26,7 +30,7 @@ def tile_picked_joinduelrangethree_none_p_kernel(
     nc = tc.nc
     with ExitStack() as ctx:
         keep = ctx.enter_context(tc.tile_pool(name="keep", bufs=1))
-        ring = ctx.enter_context(tc.tile_pool(name="ring", bufs=2))
+        ring = ctx.enter_context(tc.tile_pool(name="ring", bufs=4))
         psum = ctx.enter_context(tc.psum_pool(name="psum", bufs=1))
 
         def load_list(name, dram):
@@ -35,14 +39,14 @@ def tile_picked_joinduelrangethree_none_p_kernel(
             return tile
 
         def load_weight(name, dram, c0, c1):
-            tile = keep.tile([P, PACK, c1 - c0], F32, name=name)
+            tile = keep.tile([P, PACK, c1 - c0], F32, name=name, tag=name, align_bytes=64)
             nc.sync.dma_start(tile[:], dram.rearrange("(p j) c -> p j c", j=PACK)[:, :, c0:c1])
             return tile
 
-        def deal(engine_copy, grouped, raw, c0, c1):
+        def deal(engine_copy, grouped, raw, c0, c1, first=0):
             engine_copy(
                 out=grouped[:].rearrange("p (t m j) -> p m j t", t=PACK, j=PACK)[:, c0 // PACK : c1 // PACK],
-                in_=raw[:].rearrange("p j (m t) -> p m j t", t=PACK),
+                in_=raw[:, :, c0 - first : c1 - first].rearrange("p j (m t) -> p m j t", t=PACK),
             )
 
         def mx_tiles(name):
@@ -58,28 +62,28 @@ def tile_picked_joinduelrangethree_none_p_kernel(
                 in_=grouped[:, PACK * c0 : PACK * c1],
             )
 
-        def product(bank, w_mx, t, x_mx, start, stop):
+        def product(bank, w_mx, t, x_mx, c0, c1, start, stop):
             nc.tensor.matmul_mx(
                 out=bank[:],
                 lhsT=w_mx[0][:, t * P : (t + 1) * P].bitcast(FP8X4),
                 lhsT_scale=w_mx[1][:, t * P : (t + 1) * P],
-                rhs=x_mx[0][:].bitcast(FP8X4),
-                rhs_scale=x_mx[1][:],
+                rhs=x_mx[0][:, c0:c1].bitcast(FP8X4),
+                rhs_scale=x_mx[1][:, c0:c1],
                 start=start,
                 stop=stop,
             )
 
         x_bytes = keep.tile([P, T], U8, name="x_bytes")
-        nc.vector.memset(x_bytes[:].bitcast(I32), 0)
+        nc.gpsimd.memset(x_bytes[:].bitcast(I32), 0)
         offs_t = load_list("offs_t", offs)
         x_table = keep.tile([P, T], U32, name="x_table")
         nc.sync.dma_start(x_table[:].bitcast(I32), x_words[0].rearrange("p n t -> p (n t)").bitcast(I32))
         for q in range(4):
-            nc.scalar.dma_start(
+            nc.sync.dma_start(
                 x_bytes[32 * q : 32 * q + 4, :].bitcast(I32), x_scales[0][4 * q : 4 * q + 4, :].bitcast(I32)
             )
-        w1_a = load_weight("w1_a", w1, 0, H // 2)
-        w1_b = load_weight("w1_b", w1, H // 2, H)
+        w1_a = load_weight("w1_a", w1, 0, W1_SPLIT)
+        w1_b = load_weight("w1_b", w1, W1_SPLIT, H)
         n1_t = load_list("n1_t", n1)
         n2_t = load_list("n2_t", n2)
         n3_t = load_list("n3_t", n3)
@@ -91,95 +95,228 @@ def tile_picked_joinduelrangethree_none_p_kernel(
         n5_t = load_list("n5_t", n5)
         n6_t = load_list("n6_t", n6)
         n7_t = load_list("n7_t", n7)
-        w3_raw = load_weight("w3_raw", w3, 0, N)
-        w2_raw = load_weight("w2_raw", w2, 0, N)
+        w3_raw = load_weight("w_raw", w3, 0, N)
 
         win_a = [keep.tile([P, WINDOW], F32, name="win_a%d" % t) for t in range(PACK)]
-        win_b = [keep.tile([P, WINDOW], F32, name="win_b%d" % t) for t in range(PACK)]
+        win_b = [keep.tile([P, WINDOW], F32, name="win_b%d" % t) for t in range(PACK - 1)]
+        win_b.append(keep.tile([P, S + 2 * S], F32, name="win_b3", align_bytes=64))
         for t in range(PACK):
-            nc.vector.memset(win_a[t][:, S:], 0.0)
-        for t in range(PACK):
-            nc.vector.memset(win_b[t][:, S:], 0.0)
+            nc.gpsimd.memset(win_a[t][:, S:], 0.0)
+        ident = keep.tile([P, P], F32, name="ident")
+        make_identity(nc, ident[:])
 
         x_mx = mx_tiles("x")
-        nc.vector.tensor_copy(x_mx[1][:], x_bytes[:].indirect(offs_t[:]))
         nc.vector.tensor_copy(x_mx[0][:], x_table[:].indirect(offs_t[:]))
+        nc.vector.tensor_copy(x_mx[1][:], x_bytes[:].indirect(offs_t[:]))
 
         w1_g = keep.tile([P, PACK * H], BF16, name="w1_g", align_bytes=64)
-        deal(nc.scalar.copy, w1_g, w1_a, 0, H // 2)
-        deal(nc.vector.tensor_copy, w1_g, w1_b, H // 2, H)
+        deal(nc.scalar.copy, w1_g, w1_a, 0, W1_SPLIT)
+        deal(nc.vector.tensor_copy, w1_g, w1_b, W1_SPLIT, W1_VECTOR_END, W1_SPLIT)
+        deal(nc.scalar.copy, w1_g, w1_b, W1_VECTOR_END, H, W1_SPLIT)
         w1_mx = mx_tiles("w1")
-        y_plain = []
         for t in range(PACK):
             quantize(w1_mx, w1_g, t * P, (t + 1) * P)
-            bank = psum.tile([P, S], F32, name="y_bank%d" % t)
-            product(bank, w1_mx, t, x_mx, True, True)
-            nc.scalar.copy(out=win_a[t][:, :S], in_=bank[:])
-            plain = keep.tile([P, S], F32, name="y_plain%d" % t)
-            nc.scalar.copy(out=plain[:], in_=bank[:])
-            y_plain.append(plain)
+            if t == 0:
+                left = psum.tile([P, HALF], F32, name="y_left", tag="a0")
+                right = psum.tile([P, HALF], F32, name="y_right", tag="b0")
+                product(left, w1_mx, t, x_mx, 0, HALF, True, True)
+                product(right, w1_mx, t, x_mx, HALF, S, True, True)
+                nc.scalar.copy(out=win_a[t][:, :HALF], in_=left[:])
+                nc.vector.tensor_copy(out=win_a[t][:, HALF:S], in_=right[:])
+            else:
+                bank = psum.tile([P, S], F32, name="y_bank", tag="a%d" % t)
+                product(bank, w1_mx, t, x_mx, 0, S, True, True)
+                nc.scalar.copy(out=win_a[t][:, :S], in_=bank[:])
 
-        z_g = keep.tile([P, PACK * S], BF16, name="z_g", align_bytes=64)
-        z2_g = keep.tile([P, PACK * S], BF16, name="z2_g", align_bytes=64)
-        z_view = z_g[:].rearrange("p (j t) -> p j t", t=PACK)
-        z2_view = z2_g[:].rearrange("p (j t) -> p j t", t=PACK)
+        pair_a = keep.tile([P, PACK, W], F32, name="pair_a")
+        pair_b = keep.tile([P, PACK, W], F32, name="pair_b")
+        for t in range(PACK):
+            nc.vector.tensor_copy(pair_a[:, t, :], win_a[t][:].indirect(n1_t[:]))
+            nc.vector.tensor_copy(pair_b[:, t, :], win_a[t][:].indirect(n2_t[:]))
+        plain = [keep.tile([P, S], F32, name="plain%d" % t) for t in range(PACK)]
+        nc.scalar.copy(out=plain[0][:], in_=win_a[0][:, :S])
+        for t in range(1, PACK):
+            nc.sync.dma_start(plain[t][:], win_a[t][:, :S])
+        w2_raw = load_weight("w1_codes", w2, 0, N)
+        half_gm = keep.tile([P, PACK], F32, name="half_gm")
+        nc.scalar.activation(half_gm[:], gm_t[:], ACT.Copy, scale=0.5)
+        neg_half_gm = keep.tile([P, PACK], F32, name="neg_half_gm")
+        nc.scalar.activation(neg_half_gm[:], gm_t[:], ACT.Copy, scale=-0.5)
+
+        d1 = [keep.tile([P, S], F32, name="d1_%d" % t)[:] for t in range(PACK - 1)] + [win_b[0][:, S:]]
+        d2 = [keep.tile([P, S], F32, name="d2_%d" % t)[:] for t in range(PACK - 2)] + [win_b[2][:, S:], win_b[1][:, S:]]
+        sums = [psum.tile([P, PACK, P], F32, name="sums", tag="b%d" % c) for c in range(PACK)]
+        sig_a = keep.tile([P, PACK, W], F32, name="sig_a")
+        sig_b = keep.tile([P, PACK, W], F32, name="sig_b")
         w2_g = keep.tile([P, PACK * N], BF16, name="w2_g", align_bytes=64)
         w3_g = keep.tile([P, PACK * N], BF16, name="w3_g", align_bytes=64)
 
+        deal(nc.scalar.copy, w3_g, w3_raw, 0, N)
+        own = [keep.tile([P, S], F32, name="own%d" % t) for t in range(PACK)]
         for t in range(PACK):
-            y_win = win_a[t]
-            pair = ring.tile([P, 2, W], F32, name="pair")
-            nc.vector.tensor_copy(pair[:, 0, :], y_win[:].indirect(n1_t[:]))
-            nc.vector.tensor_copy(pair[:, 1, :], y_win[:].indirect(n2_t[:]))
-            diff = ring.tile([P, W], F32, name="diff")
-            nc.vector.tensor_tensor(diff[:], pair[:, 0, :], pair[:, 1, :], ALU.subtract)
-            sig = ring.tile([P, 2, W], F32, name="sig")
-            nc.scalar.activation(sig[:, 0, :], diff[:], ACT.Sigmoid)
-            nc.scalar.activation(sig[:, 1, :], diff[:], ACT.Sigmoid, scale=-1.0)
+            nc.scalar.activation(own[t][:], win_a[t][:, :S], ACT.Copy, scale=half_gm[:, t : t + 1])
 
-            d1 = ring.tile([P, S], F32, name="d1")
-            d2 = ring.tile([P, S], F32, name="d2")
-            nc.vector.tensor_tensor(d1[:], y_win[:].indirect(n3_t[:]), y_plain[t][:], ALU.subtract)
-            nc.vector.tensor_tensor(d2[:], y_win[:].indirect(n4_t[:]), y_plain[t][:], ALU.subtract)
+        def gates():
+            neg_b = keep.tile([P, PACK, W], F32, name="neg_b")
+            nc.scalar.activation(neg_b[:], pair_b[:], ACT.Copy, scale=-1.0)
+            turned = keep.tile([P, 2, PACK, P], F32, name="turned")
+            for c in range(2):
+                bank = psum.tile([P, PACK, P], F32, name="diff_turned", tag="a%d" % c)
+                for t in range(PACK):
+                    for i, term in enumerate((pair_a, neg_b)):
+                        nc.tensor.matmul(
+                            bank[:, t, :], lhsT=term[:, t, c * P : (c + 1) * P], rhs=ident[:],
+                            is_transpose=True, start=(i == 0), stop=(i == 1),
+                        )
+                nc.scalar.copy(out=turned[:, c], in_=bank[:])
+            for tt in range(2):
+                bank = psum.tile([P, 2, W], F32, name="diff", tag="a%d" % (2 + tt))
+                for t2 in range(2):
+                    for c in range(2):
+                        nc.tensor.transpose(bank[:, t2, c * P : (c + 1) * P], turned[:, c, 2 * tt + t2, :], ident[:])
+                nc.scalar.activation(sig_a[:, 2 * tt : 2 * tt + 2, :], bank[:], ACT.Sigmoid)
+                nc.scalar.activation(sig_b[:, 2 * tt : 2 * tt + 2, :], bank[:], ACT.Sigmoid, scale=-1.0)
+
+        def extremes(t):
             hi = ring.tile([P, S], F32, name="hi")
             lo = ring.tile([P, S], F32, name="lo")
-            nc.vector.tensor_tensor(win_b[t][:].indirect(n1_t[:]), pair[:, 0, :], sig[:, 0, :], ALU.mult)
-            nc.vector.scalar_tensor_tensor(hi[:], d1[:], 0.0, d2[:], ALU.max, ALU.max)
-            nc.vector.scalar_tensor_tensor(lo[:], d1[:], 0.0, d2[:], ALU.min, ALU.min)
-            part = ring.tile([P, S], F32, name="part")
-            nc.vector.scalar_tensor_tensor(part[:], y_plain[t][:], 0.5, hi[:], ALU.mult, ALU.add)
-            rng = ring.tile([P, S], F32, name="rng")
-            nc.vector.scalar_tensor_tensor(rng[:], lo[:], -0.5, part[:], ALU.mult, ALU.add)
-            nc.vector.tensor_tensor(win_b[t][:].indirect(n2_t[:]), pair[:, 1, :], sig[:, 1, :], ALU.mult)
-            nc.scalar.activation(z2_view[:, :, t], rng[:], ACT.Copy, scale=gm_t[:, t : t + 1])
-            nc.scalar.activation(z_view[:, :, t], win_b[t][:, :S], ACT.Copy, scale=gn_t[:, t : t + 1])
+            nc.vector.scalar_tensor_tensor(hi[:], d1[t], 0.0, d2[t], ALU.max, ALU.max)
+            nc.vector.scalar_tensor_tensor(lo[:], d1[t], 0.0, d2[t], ALU.min, ALU.min)
+            terms = [own[t]] + [ring.tile([P, S], F32, name="term%d" % i) for i in range(2)]
+            nc.scalar.activation(terms[1][:], hi[:], ACT.Copy, scale=gm_t[:, t : t + 1])
+            nc.scalar.activation(terms[2][:], lo[:], ACT.Copy, scale=neg_half_gm[:, t : t + 1])
+            for c in range(PACK):
+                for i in range(3):
+                    nc.tensor.matmul(
+                        sums[c][:, t, :], lhsT=terms[i][:, c * P : (c + 1) * P], rhs=ident[:],
+                        is_transpose=True, start=(i == 0), stop=(i == 2),
+                    )
+
+        for t in range(PACK):
+            nc.vector.tensor_tensor(d1[t], win_a[t][:].indirect(n3_t[:]), plain[t][:], ALU.subtract)
+            if t == 0:
+                gates()
+            else:
+                extremes(t - 1)
+            nc.vector.tensor_tensor(d2[t], win_a[t][:].indirect(n4_t[:]), plain[t][:], ALU.subtract)
             if t == 1:
-                deal(nc.scalar.copy, w3_g, w3_raw, 0, N)
-            if t == 2:
                 deal(nc.scalar.copy, w2_g, w2_raw, 0, N)
+
+        def put(lst, pair, sig, t):
+            nc.vector.tensor_tensor(win_b[t][:].indirect(lst[:]), pair[:, t, :], sig[:, t, :], ALU.mult)
+
+        z_g = [keep.tile([P, PACK * HALF], BF16, name="z_g%d" % b, tag="z_g%d" % b, align_bytes=64) for b in range(2)]
+        z_view = [g[:].rearrange("p (j t) -> p j t", t=PACK) for g in z_g]
+
+        def round_z_scalar(t, b):
+            nc.scalar.activation(
+                z_view[b][:, :, t], win_b[t][:, b * HALF : (b + 1) * HALF], ACT.Copy, scale=gn_t[:, t : t + 1]
+            )
+
+        def round_z_vector(t, b):
+            nc.vector.tensor_scalar(
+                z_view[b][:, :, t], win_b[t][:, b * HALF : (b + 1) * HALF], gn_t[:, t : t + 1], None, ALU.mult
+            )
+
+        def quantize_z(b):
+            cols = slice(b * HALF, (b + 1) * HALF)
+            nc.vector.quantize_mx(out=z_mx[0][:, cols].bitcast(FP8X4), scales=z_mx[1][:, cols], in_=z_g[b][:])
 
         w2_mx, w3_mx, z_mx, z2_mx = mx_tiles("w2"), mx_tiles("w3"), mx_tiles("z"), mx_tiles("z2")
         quantize(w3_mx, w3_g, 0, N)
-        quantize(w2_mx, w2_g, 0, N)
-        quantize(z2_mx, z2_g, 0, S)
-        quantize(z_mx, z_g, 0, S)
-        banks = [psum.tile([P, S], F32, name="h_bank%d" % t) for t in range(PACK)]
-        for t in range(PACK):
-            product(banks[t], w3_mx, t, z2_mx, True, False)
-        for t in range(PACK):
-            product(banks[t], w2_mx, t, z_mx, False, True)
+        extremes(PACK - 1)
+        for t in range(PACK - 1):
+            put(n1_t, pair_a, sig_a, t)
+        for t in range(PACK - 1):
+            put(n2_t, pair_b, sig_b, t)
 
-        for t in range(PACK):
-            nc.scalar.copy(out=win_a[t][:, :S], in_=banks[t][:])
-            nc.scalar.copy(out=y_plain[t][:], in_=banks[t][:])
-            nc.vector.tensor_tensor(win_b[t][:, :S], win_a[t][:].indirect(n5_t[:]), y_plain[t][:], ALU.subtract)
-        for t in range(PACK):
-            far = ring.tile([P, S], F32, name="far")
-            nc.vector.tensor_copy(far[:], win_b[t][:].indirect(n6_t[:]))
-            nc.vector.tensor_tensor(y_plain[t][:], win_b[t][:, :S], far[:], ALU.min)
-            nc.scalar.activation(win_a[t][:, :S], y_plain[t][:], ACT.Copy, scale=-0.5)
+        for cc in range(2):
+            words = psum.tile([P, 2, 2, P], F32, name="words", tag="a%d" % (cc + 1))
+            for c2 in range(2):
+                rows = z_g[1 - c2][:, cc * H : (cc + 1) * H]
+                nc.scalar.copy(
+                    out=rows.rearrange("j (u p e) -> j u p e", u=2, e=2),
+                    in_=sums[2 * cc + c2][:].rearrange("j (u e) p -> j u p e", u=2),
+                )
+                for u in range(2):
+                    nc.tensor.transpose(words[:, c2, u, :], rows.bitcast(F32)[:, u * P : (u + 1) * P], ident[:])
+            nc.scalar.copy(
+                out=win_b[3][:, (1 + cc) * S : (2 + cc) * S].rearrange("p (c j u) -> p c j u", c=2, u=2),
+                in_=words[:].rearrange("p c u j -> p c j u"),
+            )
+        nc.vector.quantize_mx(out=z2_mx[0][:].bitcast(FP8X4), scales=z2_mx[1][:], in_=win_b[3][:, S:].bitcast(BF16))
+
+        for t in range(2):
+            for b in range(2):
+                round_z_scalar(t, b)
+        round_z_scalar(2, 0)
+        put(n1_t, pair_a, sig_a, 3)
+        parts = ((HALF, S, "b0"), (0, HALF, "a0"))
+        h_first = [psum.tile([P, c1 - c0], F32, name="h_first", tag=tag) for c0, c1, tag in parts]
+        banks = [psum.tile([P, S], F32, name="h_bank", tag="b%d" % t) for t in range(1, PACK)]
+        for bank, (c0, c1, tag) in zip(h_first, parts):
+            product(bank, w3_mx, 0, z2_mx, c0, c1, True, False)
+        for t in range(1, PACK):
+            product(banks[t - 1], w3_mx, t, z2_mx, 0, S, True, False)
+        round_z_vector(2, 1)
+        quantize(w2_mx, w2_g, 0, P)
+        put(n2_t, pair_b, sig_b, 3)
+        round_z_scalar(3, 0)
+        round_z_vector(3, 1)
+        quantize_z(1)
+        product(h_first[0], w2_mx, 0, z_mx, HALF, S, False, True)
+        quantize_z(0)
+        product(h_first[1], w2_mx, 0, z_mx, 0, HALF, False, True)
+        late_codes = keep.tile([P, N], U32, name="late_codes", tag="z_g0", align_bytes=64)
+        w2_late = (late_codes, w2_mx[1])
+        quantize(w2_late, w2_g, P, 2 * P)
+        quantize(w2_late, w2_g, 2 * P, N)
+        for t in range(1, PACK):
+            product(banks[t - 1], w2_late, t, z_mx, 0, S, False, True)
+
+        for bank, (c0, c1, tag), engine_copy in zip(
+            h_first, parts, (nc.scalar.copy, nc.vector.tensor_copy)
+        ):
+            engine_copy(out=win_a[0][:, c0:c1], in_=bank[:])
+            engine_copy(out=plain[0][:, c0:c1], in_=bank[:])
+        for t in range(1, PACK):
+            nc.scalar.copy(out=win_a[t][:, :S], in_=banks[t - 1][:])
+            nc.scalar.copy(out=plain[t][:], in_=banks[t - 1][:])
+
         out_rows = out.rearrange("(p t) n -> p t n", t=PACK)
-        for t in range(PACK):
-            result = keep.tile([P, S], F32, name="result%d" % t)
-            nc.vector.tensor_tensor(result[:], win_a[t][:].indirect(n7_t[:]), y_plain[t][:], ALU.subtract)
-            nc.sync.dma_start(out_rows[:, t, :], result[:])
+
+        def step(t):
+            nc.vector.tensor_tensor(win_b[t][:, :S], win_a[t][:].indirect(n5_t[:]), plain[t][:], ALU.subtract)
+
+        def fetch(t):
+            nc.vector.tensor_copy(d1[t], win_b[t][:].indirect(n6_t[:]))
+
+        def least(t):
+            nc.vector.tensor_tensor(plain[t][:], win_b[t][:, :S], d1[t], ALU.min)
+            nc.scalar.activation(win_a[t][:, :S], plain[t][:], ACT.Copy, scale=-0.5)
+
+        def finish(t):
+            nc.vector.tensor_tensor(d2[t], win_a[t][:].indirect(n7_t[:]), plain[t][:], ALU.subtract)
+            nc.sync.dma_start(out_rows[:, t, :], d2[t])
+
+        step(0)
+        step(1)
+        fetch(0)
+        step(2)
+        least(0)
+        fetch(1)
+        step(3)
+        least(1)
+        fetch(2)
+        finish(0)
+        least(2)
+        fetch(3)
+        finish(1)
+        least(3)
+        finish(2)
+        for c0 in (0, HALF):
+            cols = slice(c0, c0 + HALF)
+            nc.vector.tensor_tensor(
+                d2[3][:, cols], win_a[3][:].indirect(n7_t[:, c0 // 16 : (c0 + HALF) // 16]), plain[3][:, cols], ALU.subtract
+            )
+            nc.sync.dma_start(out_rows[:, 3, cols], d2[3][:, cols])

@@ -99,13 +99,15 @@ def tile_picked_joinduelrangethree_none_p_kernel(
 
         win_a = [keep.tile([P, WINDOW], F32, name="win_a%d" % t) for t in range(PACK)]
         win_b = [keep.tile([P, WINDOW], F32, name="win_b%d" % t) for t in range(PACK - 1)]
-        win_b.append(keep.tile([P, S + 2 * S], F32, name="win_b3", align_bytes=64))
+        win_b.append(keep.tile([P, 3 * S + PACK], F32, name="win_b3", align_bytes=64))
         for t in range(PACK):
             nc.gpsimd.memset(win_a[t][:, S:], 0.0)
         ident = keep.tile([P, P], F32, name="ident")
         make_identity(nc, ident[:])
 
         x_mx = mx_tiles("x")
+        warm = keep.tile([P, 1], F32, name="warm")
+        nc.scalar.activation(warm[:], win_a[0][:, S : S + 1], ACT.Sigmoid)
         nc.vector.tensor_copy(x_mx[0][:], x_table[:].indirect(offs_t[:]))
         nc.vector.tensor_copy(x_mx[1][:], x_bytes[:].indirect(offs_t[:]))
 
@@ -138,16 +140,18 @@ def tile_picked_joinduelrangethree_none_p_kernel(
         for t in range(1, PACK):
             nc.sync.dma_start(plain[t][:], win_a[t][:, :S])
         w2_raw = load_weight("w1_codes", w2, 0, N)
+        gn_held = win_b[3][:, 3 * S :]
+        nc.scalar.copy(out=gn_held, in_=gn_t[:])
         half_gm = keep.tile([P, PACK], F32, name="half_gm")
         nc.scalar.activation(half_gm[:], gm_t[:], ACT.Copy, scale=0.5)
         neg_half_gm = keep.tile([P, PACK], F32, name="neg_half_gm")
         nc.scalar.activation(neg_half_gm[:], gm_t[:], ACT.Copy, scale=-0.5)
 
-        d1 = [keep.tile([P, S], F32, name="d1_%d" % t)[:] for t in range(PACK - 1)] + [win_b[0][:, S:]]
-        d2 = [keep.tile([P, S], F32, name="d2_%d" % t)[:] for t in range(PACK - 2)] + [win_b[2][:, S:], win_b[1][:, S:]]
+        d1 = [keep.tile([P, S], F32, name="d1_%d" % t)[:] for t in range(PACK - 1)] + [win_b[2][:, S:]]
+        d2 = [keep.tile([P, S], F32, name="d2_%d" % t)[:] for t in range(PACK - 2)] + [win_b[1][:, S:], win_b[0][:, S:]]
         sums = [psum.tile([P, PACK, P], F32, name="sums", tag="b%d" % c) for c in range(PACK)]
         sig_a = keep.tile([P, PACK, W], F32, name="sig_a")
-        sig_b = keep.tile([P, PACK, W], F32, name="sig_b")
+        sig_b = keep.tile([P, PACK, W], F32, name="sig_b", tag="sig_b", align_bytes=64)
         w2_g = keep.tile([P, PACK * N], BF16, name="w2_g", align_bytes=64)
         w3_g = keep.tile([P, PACK * N], BF16, name="w3_g", align_bytes=64)
 
@@ -208,9 +212,9 @@ def tile_picked_joinduelrangethree_none_p_kernel(
         z_g = [keep.tile([P, PACK * HALF], BF16, name="z_g%d" % b, tag="z_g%d" % b, align_bytes=64) for b in range(2)]
         z_view = [g[:].rearrange("p (j t) -> p j t", t=PACK) for g in z_g]
 
-        def round_z_scalar(t, b):
+        def round_z_scalar(t, b, gains):
             nc.scalar.activation(
-                z_view[b][:, :, t], win_b[t][:, b * HALF : (b + 1) * HALF], ACT.Copy, scale=gn_t[:, t : t + 1]
+                z_view[b][:, :, t], win_b[t][:, b * HALF : (b + 1) * HALF], ACT.Copy, scale=gains[:, t : t + 1]
             )
 
         def round_z_vector(t, b):
@@ -222,12 +226,13 @@ def tile_picked_joinduelrangethree_none_p_kernel(
             cols = slice(b * HALF, (b + 1) * HALF)
             nc.vector.quantize_mx(out=z_mx[0][:, cols].bitcast(FP8X4), scales=z_mx[1][:, cols], in_=z_g[b][:])
 
-        w2_mx, w3_mx, z_mx, z2_mx = mx_tiles("w2"), mx_tiles("w3"), mx_tiles("z"), mx_tiles("z2")
+        w3_mx, z_mx, z2_mx = mx_tiles("w3"), mx_tiles("z"), mx_tiles("z2")
+        w2_scales = keep.tile([P, N], U8, name="w2_scales", align_bytes=64)
         quantize(w3_mx, w3_g, 0, N)
         extremes(PACK - 1)
-        for t in range(PACK - 1):
+        for t in (2, 0, 1):
             put(n1_t, pair_a, sig_a, t)
-        for t in range(PACK - 1):
+        for t in (2, 0, 1):
             put(n2_t, pair_b, sig_b, t)
 
         for cc in range(2):
@@ -244,12 +249,13 @@ def tile_picked_joinduelrangethree_none_p_kernel(
                 out=win_b[3][:, (1 + cc) * S : (2 + cc) * S].rearrange("p (c j u) -> p c j u", c=2, u=2),
                 in_=words[:].rearrange("p c u j -> p c j u"),
             )
-        nc.vector.quantize_mx(out=z2_mx[0][:].bitcast(FP8X4), scales=z2_mx[1][:], in_=win_b[3][:, S:].bitcast(BF16))
+        nc.vector.quantize_mx(out=z2_mx[0][:].bitcast(FP8X4), scales=z2_mx[1][:], in_=win_b[3][:, S : 3 * S].bitcast(BF16))
 
+        round_z_scalar(2, 1, gn_held)
+        round_z_scalar(2, 0, gn_t)
         for t in range(2):
             for b in range(2):
-                round_z_scalar(t, b)
-        round_z_scalar(2, 0)
+                round_z_scalar(t, b, gn_t)
         put(n1_t, pair_a, sig_a, 3)
         parts = ((HALF, S, "b0"), (0, HALF, "a0"))
         h_first = [psum.tile([P, c1 - c0], F32, name="h_first", tag=tag) for c0, c1, tag in parts]
@@ -258,27 +264,27 @@ def tile_picked_joinduelrangethree_none_p_kernel(
             product(bank, w3_mx, 0, z2_mx, c0, c1, True, False)
         for t in range(1, PACK):
             product(banks[t - 1], w3_mx, t, z2_mx, 0, S, True, False)
-        round_z_vector(2, 1)
-        quantize(w2_mx, w2_g, 0, P)
         put(n2_t, pair_b, sig_b, 3)
-        round_z_scalar(3, 0)
+        round_z_scalar(3, 0, gn_t)
         round_z_vector(3, 1)
+        first_codes = keep.tile([P, P], U32, name="first_codes", tag="sig_b", align_bytes=64)
+        w2_first = (first_codes, w2_scales)
+        quantize(w2_first, w2_g, 0, P)
         quantize_z(1)
-        product(h_first[0], w2_mx, 0, z_mx, HALF, S, False, True)
+        product(h_first[0], w2_first, 0, z_mx, HALF, S, False, True)
         quantize_z(0)
-        product(h_first[1], w2_mx, 0, z_mx, 0, HALF, False, True)
+        product(h_first[1], w2_first, 0, z_mx, 0, HALF, False, True)
         late_codes = keep.tile([P, N], U32, name="late_codes", tag="z_g0", align_bytes=64)
-        w2_late = (late_codes, w2_mx[1])
+        w2_late = (late_codes, w2_scales)
         quantize(w2_late, w2_g, P, 2 * P)
         quantize(w2_late, w2_g, 2 * P, N)
         for t in range(1, PACK):
             product(banks[t - 1], w2_late, t, z_mx, 0, S, False, True)
 
-        for bank, (c0, c1, tag), engine_copy in zip(
-            h_first, parts, (nc.scalar.copy, nc.vector.tensor_copy)
-        ):
-            engine_copy(out=win_a[0][:, c0:c1], in_=bank[:])
-            engine_copy(out=plain[0][:, c0:c1], in_=bank[:])
+        nc.scalar.copy(out=win_a[0][:, HALF:S], in_=h_first[0][:])
+        nc.scalar.copy(out=plain[0][:, HALF:S], in_=h_first[0][:])
+        nc.vector.tensor_copy(out=win_a[0][:, :HALF], in_=h_first[1][:])
+        nc.vector.tensor_copy(out=plain[0][:, :HALF], in_=h_first[1][:])
         for t in range(1, PACK):
             nc.scalar.copy(out=win_a[t][:, :S], in_=banks[t - 1][:])
             nc.scalar.copy(out=plain[t][:], in_=banks[t - 1][:])

@@ -106,8 +106,6 @@ def tile_picked_joinduelrangethree_none_p_kernel(
         make_identity(nc, ident[:])
 
         x_mx = mx_tiles("x")
-        warm = keep.tile([P, 1], F32, name="warm")
-        nc.scalar.activation(warm[:], win_a[0][:, S : S + 1], ACT.Sigmoid)
         nc.vector.tensor_copy(x_mx[0][:], x_table[:].indirect(offs_t[:]))
         nc.vector.tensor_copy(x_mx[1][:], x_bytes[:].indirect(offs_t[:]))
 

from contextlib import ExitStack

import concourse.mybir as mybir
from concourse.masks import make_identity

K, T, S, H, N, W = 512, 2048, 512, 512, 512, 256
FLOPS = 2 * S * (K * H + 2 * H * N)

F32 = mybir.dt.float32
BF16 = mybir.dt.bfloat16
I32 = mybir.dt.int32
U32 = mybir.dt.uint32
U16 = mybir.dt.uint16
U8 = mybir.dt.uint8
FP8X4 = mybir.dt.float8_e4m3fn_x4
ALU = mybir.AluOpType
ACT = mybir.ActivationFunctionType

P = 128
PACK = 4
WINDOW = 2 * S
HALF = S // 2
W1_SPLIT = 256
W1_VECTOR_END = 416


def tile_picked_joinduelrangethree_none_p_kernel(
    tc, x_words, x_scales, w1, gn, gm, w2, w3, offs, n1, n2, n3, n4, n5, n6, n7, out
):
    nc = tc.nc
    with ExitStack() as ctx:
        keep = ctx.enter_context(tc.tile_pool(name="keep", bufs=1))
        ring = ctx.enter_context(tc.tile_pool(name="ring", bufs=4))
        psum = ctx.enter_context(tc.psum_pool(name="psum", bufs=1))

        def load_list(name, dram):
            tile = keep.tile(list(dram.shape), U16, name=name)
            nc.sync.dma_start(tile[:], dram)
            return tile

        def load_weight(name, dram, c0, c1):
            tile = keep.tile([P, PACK, c1 - c0], F32, name=name, tag=name, align_bytes=64)
            nc.sync.dma_start(tile[:], dram.rearrange("(p j) c -> p j c", j=PACK)[:, :, c0:c1])
            return tile

        def deal(engine_copy, grouped, raw, c0, c1, first=0):
            engine_copy(
                out=grouped[:].rearrange("p (t m j) -> p m j t", t=PACK, j=PACK)[:, c0 // PACK : c1 // PACK],
                in_=raw[:, :, c0 - first : c1 - first].rearrange("p j (m t) -> p m j t", t=PACK),
            )

        def mx_tiles(name):
            return (
                keep.tile([P, S], U32, name=name + "_codes", align_bytes=64),
                keep.tile([P, S], U8, name=name + "_scales", align_bytes=64),
            )

        def quantize(mx, grouped, c0, c1):
            nc.vector.quantize_mx(
                out=mx[0][:, c0:c1].bitcast(FP8X4),
                scales=mx[1][:, c0:c1],
                in_=grouped[:, PACK * c0 : PACK * c1],
            )

        def product(bank, w_mx, t, x_mx, c0, c1, start, stop):
            nc.tensor.matmul_mx(
                out=bank[:],
                lhsT=w_mx[0][:, t * P : (t + 1) * P].bitcast(FP8X4),
                lhsT_scale=w_mx[1][:, t * P : (t + 1) * P],
                rhs=x_mx[0][:, c0:c1].bitcast(FP8X4),
                rhs_scale=x_mx[1][:, c0:c1],
                start=start,
                stop=stop,
            )

        x_bytes = keep.tile([P, T], U8, name="x_bytes")
        nc.gpsimd.memset(x_bytes[:].bitcast(I32), 0)
        offs_t = load_list("offs_t", offs)
        x_table = keep.tile([P, T], U32, name="x_table")
        nc.sync.dma_start(x_table[:].bitcast(I32), x_words[0].rearrange("p n t -> p (n t)").bitcast(I32))
        for q in range(4):
            nc.sync.dma_start(
                x_bytes[32 * q : 32 * q + 4, :].bitcast(I32), x_scales[0][4 * q : 4 * q + 4, :].bitcast(I32)
            )
        w1_a = load_weight("w1_a", w1, 0, W1_SPLIT)
        w1_b = load_weight("w1_b", w1, W1_SPLIT, H)
        n1_t = load_list("n1_t", n1)
        n2_t = load_list("n2_t", n2)
        n3_t = load_list("n3_t", n3)
        n4_t = load_list("n4_t", n4)
        gn_t = keep.tile([P, PACK], F32, name="gn_t")
        nc.sync.dma_start(gn_t[:], gn.rearrange("(p t) one -> p (t one)", t=PACK))
        gm_t = keep.tile([P, PACK], F32, name="gm_t")
        nc.sync.dma_start(gm_t[:], gm.rearrange("(p t) one -> p (t one)", t=PACK))
        n5_t = load_list("n5_t", n5)
        n6_t = load_list("n6_t", n6)
        n7_t = load_list("n7_t", n7)
        w3_raw = load_weight("w_raw", w3, 0, N)

        win_a = [keep.tile([P, WINDOW], F32, name="win_a%d" % t) for t in range(PACK)]
        win_b = [keep.tile([P, WINDOW], F32, name="win_b%d" % t) for t in range(PACK - 1)]
        win_b.append(keep.tile([P, 3 * S + PACK], F32, name="win_b3", align_bytes=64))
        for t in range(PACK):
            nc.gpsimd.memset(win_a[t][:, S:], 0.0)
        ident = keep.tile([P, P], F32, name="ident")
        make_identity(nc, ident[:])

        x_mx = mx_tiles("x")
        nc.vector.tensor_copy(x_mx[0][:], x_table[:].indirect(offs_t[:]))
        nc.vector.tensor_copy(x_mx[1][:], x_bytes[:].indirect(offs_t[:]))

        w1_g = keep.tile([P, PACK * H], BF16, name="w1_g", align_bytes=64)
        deal(nc.scalar.copy, w1_g, w1_a, 0, W1_SPLIT)
        deal(nc.vector.tensor_copy, w1_g, w1_b, W1_SPLIT, W1_VECTOR_END, W1_SPLIT)
        deal(nc.scalar.copy, w1_g, w1_b, W1_VECTOR_END, H, W1_SPLIT)
        w1_mx = mx_tiles("w1")
        for t in range(PACK):
            quantize(w1_mx, w1_g, t * P, (t + 1) * P)
            if t == 0:
                left = psum.tile([P, HALF], F32, name="y_left", tag="a0")
                right = psum.tile([P, HALF], F32, name="y_right", tag="b0")
                product(left, w1_mx, t, x_mx, 0, HALF, True, True)
                product(right, w1_mx, t, x_mx, HALF, S, True, True)
                nc.scalar.copy(out=win_a[t][:, :HALF], in_=left[:])
                nc.vector.tensor_copy(out=win_a[t][:, HALF:S], in_=right[:])
            else:
                bank = psum.tile([P, S], F32, name="y_bank", tag="a%d" % t)
                product(bank, w1_mx, t, x_mx, 0, S, True, True)
                nc.scalar.copy(out=win_a[t][:, :S], in_=bank[:])

        pair_a = keep.tile([P, PACK, W], F32, name="pair_a")
        pair_b = keep.tile([P, PACK, W], F32, name="pair_b")
        for t in range(PACK):
            nc.vector.tensor_copy(pair_a[:, t, :], win_a[t][:].indirect(n1_t[:]))
            nc.vector.tensor_copy(pair_b[:, t, :], win_a[t][:].indirect(n2_t[:]))
        plain = [keep.tile([P, S], F32, name="plain%d" % t) for t in range(PACK)]
        nc.scalar.copy(out=plain[0][:], in_=win_a[0][:, :S])
        for t in range(1, PACK):
            nc.sync.dma_start(plain[t][:], win_a[t][:, :S])
        w2_raw = load_weight("w1_codes", w2, 0, N)
        gn_held = win_b[3][:, 3 * S :]
        nc.scalar.copy(out=gn_held, in_=gn_t[:])
        half_gm = keep.tile([P, PACK], F32, name="half_gm")
        nc.scalar.activation(half_gm[:], gm_t[:], ACT.Copy, scale=0.5)
        neg_half_gm = keep.tile([P, PACK], F32, name="neg_half_gm")
        nc.scalar.activation(neg_half_gm[:], gm_t[:], ACT.Copy, scale=-0.5)

        d1 = [keep.tile([P, S], F32, name="d1_%d" % t)[:] for t in range(PACK - 1)] + [win_b[2][:, S:]]
        d2 = [keep.tile([P, S], F32, name="d2_%d" % t)[:] for t in range(PACK - 2)] + [win_b[1][:, S:], win_b[0][:, S:]]
        sums = [psum.tile([P, PACK, P], F32, name="sums", tag="b%d" % c) for c in range(PACK)]
        sig_a = keep.tile([P, PACK, W], F32, name="sig_a")
        sig_b = keep.tile([P, PACK, W], F32, name="sig_b", tag="sig_b", align_bytes=64)
        w2_g = keep.tile([P, PACK * N], BF16, name="w2_g", align_bytes=64)
        w3_g = keep.tile([P, PACK * N], BF16, name="w3_g", align_bytes=64)

        deal(nc.scalar.copy, w3_g, w3_raw, 0, N)
        own = [keep.tile([P, S], F32, name="own%d" % t) for t in range(PACK)]
        for t in range(PACK):
            nc.scalar.activation(own[t][:], win_a[t][:, :S], ACT.Copy, scale=half_gm[:, t : t + 1])

        def gates():
            neg_b = keep.tile([P, PACK, W], F32, name="neg_b")
            nc.scalar.activation(neg_b[:], pair_b[:], ACT.Copy, scale=-1.0)
            turned = keep.tile([P, 2, PACK, P], F32, name="turned")
            for c in range(2):
                bank = psum.tile([P, PACK, P], F32, name="diff_turned", tag="a%d" % c)
                for t in range(PACK):
                    for i, term in enumerate((pair_a, neg_b)):
                        nc.tensor.matmul(
                            bank[:, t, :], lhsT=term[:, t, c * P : (c + 1) * P], rhs=ident[:],
                            is_transpose=True, start=(i == 0), stop=(i == 1),
                        )
                nc.scalar.copy(out=turned[:, c], in_=bank[:])
            for tt in range(2):
                bank = psum.tile([P, 2, W], F32, name="diff", tag="a%d" % (2 + tt))
                for t2 in range(2):
                    for c in range(2):
                        nc.tensor.transpose(bank[:, t2, c * P : (c + 1) * P], turned[:, c, 2 * tt + t2, :], ident[:])
                nc.scalar.activation(sig_a[:, 2 * tt : 2 * tt + 2, :], bank[:], ACT.Sigmoid)
                nc.scalar.activation(sig_b[:, 2 * tt : 2 * tt + 2, :], bank[:], ACT.Sigmoid, scale=-1.0)

        def extremes(t):
            hi = ring.tile([P, S], F32, name="hi")
            lo = ring.tile([P, S], F32, name="lo")
            nc.vector.scalar_tensor_tensor(hi[:], d1[t], 0.0, d2[t], ALU.max, ALU.max)
            nc.vector.scalar_tensor_tensor(lo[:], d1[t], 0.0, d2[t], ALU.min, ALU.min)
            terms = [own[t]] + [ring.tile([P, S], F32, name="term%d" % i) for i in range(2)]
            nc.scalar.activation(terms[1][:], hi[:], ACT.Copy, scale=gm_t[:, t : t + 1])
            nc.scalar.activation(terms[2][:], lo[:], ACT.Copy, scale=neg_half_gm[:, t : t + 1])
            for c in range(PACK):
                for i in range(3):
                    nc.tensor.matmul(
                        sums[c][:, t, :], lhsT=terms[i][:, c * P : (c + 1) * P], rhs=ident[:],
                        is_transpose=True, start=(i == 0), stop=(i == 2),
                    )

        for t in range(PACK):
            nc.vector.tensor_tensor(d1[t], win_a[t][:].indirect(n3_t[:]), plain[t][:], ALU.subtract)
            if t == 0:
                gates()
            else:
                extremes(t - 1)
            nc.vector.tensor_tensor(d2[t], win_a[t][:].indirect(n4_t[:]), plain[t][:], ALU.subtract)
            if t == 1:
                deal(nc.scalar.copy, w2_g, w2_raw, 0, N)

        def put(lst, pair, sig, t):
            nc.vector.tensor_tensor(win_b[t][:].indirect(lst[:]), pair[:, t, :], sig[:, t, :], ALU.mult)

        z_g = [keep.tile([P, PACK * HALF], BF16, name="z_g%d" % b, tag="z_g%d" % b, align_bytes=64) for b in range(2)]
        z_view = [g[:].rearrange("p (j t) -> p j t", t=PACK) for g in z_g]

        def round_z_scalar(t, b, gains):
            nc.scalar.activation(
                z_view[b][:, :, t], win_b[t][:, b * HALF : (b + 1) * HALF], ACT.Copy, scale=gains[:, t : t + 1]
            )

        def round_z_vector(t, b):
            nc.vector.tensor_scalar(
                z_view[b][:, :, t], win_b[t][:, b * HALF : (b + 1) * HALF], gn_t[:, t : t + 1], None, ALU.mult
            )

        def quantize_z(b):
            cols = slice(b * HALF, (b + 1) * HALF)
            nc.vector.quantize_mx(out=z_mx[0][:, cols].bitcast(FP8X4), scales=z_mx[1][:, cols], in_=z_g[b][:])

        w3_mx, z_mx, z2_mx = mx_tiles("w3"), mx_tiles("z"), mx_tiles("z2")
        w2_scales = keep.tile([P, N], U8, name="w2_scales", align_bytes=64)
        quantize(w3_mx, w3_g, 0, N)
        extremes(PACK - 1)
        for t in (2, 0, 1):
            put(n1_t, pair_a, sig_a, t)
        for t in (2, 0, 1):
            put(n2_t, pair_b, sig_b, t)

        for cc in range(2):
            words = psum.tile([P, 2, 2, P], F32, name="words", tag="a%d" % (cc + 1))
            for c2 in range(2):
                rows = z_g[1 - c2][:, cc * H : (cc + 1) * H]
                nc.scalar.copy(
                    out=rows.rearrange("j (u p e) -> j u p e", u=2, e=2),
                    in_=sums[2 * cc + c2][:].rearrange("j (u e) p -> j u p e", u=2),
                )
                for u in range(2):
                    nc.tensor.transpose(words[:, c2, u, :], rows.bitcast(F32)[:, u * P : (u + 1) * P], ident[:])
            nc.scalar.copy(
                out=win_b[3][:, (1 + cc) * S : (2 + cc) * S].rearrange("p (c j u) -> p c j u", c=2, u=2),
                in_=words[:].rearrange("p c u j -> p c j u"),
            )
        nc.vector.quantize_mx(out=z2_mx[0][:].bitcast(FP8X4), scales=z2_mx[1][:], in_=win_b[3][:, S : 3 * S].bitcast(BF16))

        round_z_scalar(2, 1, gn_held)
        round_z_scalar(2, 0, gn_t)
        for t in range(2):
            for b in range(2):
                round_z_scalar(t, b, gn_t)
        put(n1_t, pair_a, sig_a, 3)
        parts = ((HALF, S, "b0"), (0, HALF, "a0"))
        h_first = [psum.tile([P, c1 - c0], F32, name="h_first", tag=tag) for c0, c1, tag in parts]
        banks = [psum.tile([P, S], F32, name="h_bank", tag="b%d" % t) for t in range(1, PACK)]
        for bank, (c0, c1, tag) in zip(h_first, parts):
            product(bank, w3_mx, 0, z2_mx, c0, c1, True, False)
        for t in range(1, PACK):
            product(banks[t - 1], w3_mx, t, z2_mx, 0, S, True, False)
        put(n2_t, pair_b, sig_b, 3)
        round_z_scalar(3, 0, gn_t)
        round_z_vector(3, 1)
        first_codes = keep.tile([P, P], U32, name="first_codes", tag="sig_b", align_bytes=64)
        w2_first = (first_codes, w2_scales)
        quantize(w2_first, w2_g, 0, P)
        quantize_z(1)
        product(h_first[0], w2_first, 0, z_mx, HALF, S, False, True)
        quantize_z(0)
        product(h_first[1], w2_first, 0, z_mx, 0, HALF, False, True)
        late_codes = keep.tile([P, N], U32, name="late_codes", tag="z_g0", align_bytes=64)
        w2_late = (late_codes, w2_scales)
        quantize(w2_late, w2_g, P, 2 * P)
        quantize(w2_late, w2_g, 2 * P, N)
        for t in range(1, PACK):
            product(banks[t - 1], w2_late, t, z_mx, 0, S, False, True)

        nc.scalar.copy(out=win_a[0][:, HALF:S], in_=h_first[0][:])
        nc.scalar.copy(out=plain[0][:, HALF:S], in_=h_first[0][:])
        nc.vector.tensor_copy(out=win_a[0][:, :HALF], in_=h_first[1][:])
        nc.vector.tensor_copy(out=plain[0][:, :HALF], in_=h_first[1][:])
        for t in range(1, PACK):
            nc.scalar.copy(out=win_a[t][:, :S], in_=banks[t - 1][:])
            nc.scalar.copy(out=plain[t][:], in_=banks[t - 1][:])

        out_rows = out.rearrange("(p t) n -> p t n", t=PACK)

        def step(t):
            nc.vector.tensor_tensor(win_b[t][:, :S], win_a[t][:].indirect(n5_t[:]), plain[t][:], ALU.subtract)

        def fetch(t):
            nc.vector.tensor_copy(d1[t], win_b[t][:].indirect(n6_t[:]))

        def least(t):
            nc.vector.tensor_tensor(plain[t][:], win_b[t][:, :S], d1[t], ALU.min)
            nc.scalar.activation(win_a[t][:, :S], plain[t][:], ACT.Copy, scale=-0.5)

        def finish(t):
            nc.vector.tensor_tensor(d2[t], win_a[t][:].indirect(n7_t[:]), plain[t][:], ALU.subtract)
            nc.sync.dma_start(out_rows[:, t, :], d2[t])

        step(0)
        step(1)
        fetch(0)
        step(2)
        least(0)
        fetch(1)
        step(3)
        least(1)
        fetch(2)
        finish(0)
        least(2)
        fetch(3)
        finish(1)
        least(3)
        finish(2)
        for c0 in (0, HALF):
            cols = slice(c0, c0 + HALF)
            nc.vector.tensor_tensor(
                d2[3][:, cols], win_a[3][:].indirect(n7_t[:, c0 // 16 : (c0 + HALF) // 16]), plain[3][:, cols], ALU.subtract
            )
            nc.sync.dma_start(out_rows[:, 3, cols], d2[3][:, cols])
